import numpy as np
import ml_dtypes


def mxq(x, axis, fmt="e4m3"):
    dtype, down = {"e4m3": (ml_dtypes.float8_e4m3fn, 7), "e5m2": (ml_dtypes.float8_e5m2, 14)}[fmt]
    v = np.moveaxis(np.asarray(x, np.float32).astype(ml_dtypes.bfloat16).astype(np.float64), axis, -1)
    blocks = v.reshape(v.shape[:-1] + (-1, 32))
    amax = np.abs(blocks).max(-1, keepdims=True)
    byte = np.maximum(np.where(amax > 0, np.frexp(amax)[1] - 1 + 127, 0) - down, 1)
    scale = np.exp2(byte - 127.0)
    codes = (blocks / scale).astype(np.float32).astype(dtype).astype(np.float64)
    return np.moveaxis((codes * scale).reshape(v.shape), -1, axis)


WIDE = False


def mx_kscale(k):
    if not WIDE:
        return np.ones(k)
    levels = np.array([30, -30])
    if k % 512:
        return np.exp2(np.random.permutation(np.resize(levels, k // 32))).repeat(32)
    a = np.empty((k // 512, 16))
    for p in range(k // 512):
        a[p, :8] = np.random.permutation(np.resize(levels, 8))
        for g in range(8):
            far = levels[np.abs(levels - a[p, g]) >= 10]
            a[p, g + 8] = far[np.random.randint(len(far))]
    return np.exp2(a.ravel()).repeat(32)


def f64(x):
    return np.asarray(x).astype(np.float64)


def striped(idx):
    return np.tile(np.asarray(idx).reshape(-1, 16).T, (8, 1)).astype(np.uint16)


def unstriped(offs):
    return offs[:16].T.reshape(-1).astype(np.int64)


E2M1 = np.array([0.0, 0.5, 1.0, 1.5, 2.0, 3.0, 4.0, 6.0, -0.0, -0.5, -1.0, -1.5, -2.0, -3.0, -4.0, -6.0])


def pack_weight(w, fmt):
    k, n = w.shape
    w = f64(np.asarray(w, np.float32).astype(ml_dtypes.bfloat16)).reshape(k // 32, 32, n)
    amax = np.abs(w).max(1)
    if fmt in ("e4m3", "e5m2"):
        byte = np.frexp(amax)[1] - 1 + 127 - (7 if fmt == "e4m3" else 14)
    else:
        mant, ex = np.frexp(amax / 6.0)
        byte = np.where(mant > 0.5, ex, ex - 1) + 127
    byte = np.clip(np.where(amax > 0, byte, 1), 1, 254)
    scaled = (w * np.exp2(127.0 - byte)[:, None, :]).reshape(k, n).astype(np.float32)
    by_word = np.ascontiguousarray(scaled.reshape(k // 512, 128, 4, n).transpose(0, 1, 3, 2))
    if fmt in ("e4m3", "e5m2"):
        words = by_word.astype(ml_dtypes.float8_e4m3fn if fmt == "e4m3" else ml_dtypes.float8_e5m2).view(np.uint8)
    else:
        c = by_word.astype(ml_dtypes.float4_e2m1fn).view(np.uint8) & 0xF
        words = (c[..., 0::2] | (c[..., 1::2] << 4)).reshape(k // 512, 128, 2 * n)
    return np.ascontiguousarray(words), np.ascontiguousarray(byte.astype(np.uint8).reshape(k // 512, 16, n))


def unpack_weight(words, scales, fmt):
    g, _, n = scales.shape
    words = np.ascontiguousarray(words).reshape(g, 128, n, -1)
    if fmt in ("e4m3", "e5m2"):
        vals = words.view(ml_dtypes.float8_e4m3fn if fmt == "e4m3" else ml_dtypes.float8_e5m2).astype(np.float64)
    else:
        nib = np.empty((g, 128, n, 4), np.uint8)
        nib[..., 0::2] = words & 0xF
        nib[..., 1::2] = words >> 4
        vals = E2M1[nib]
    vals = vals * np.repeat(np.exp2(scales.astype(np.float64) - 127.0), 8, axis=1)[..., None]
    return vals.transpose(0, 1, 3, 2).reshape(g * 512, n)


K, T, J, R, O, N, L = 512, 2048, 256, 512, 128, 256, 512


def setup_inputs():
    n = np.random.standard_normal
    idx = np.random.permutation(T)[:J]
    idx2 = np.random.permutation(T)[:J]
    idx3 = np.random.permutation(T)[:J]
    idx4 = np.random.permutation(J)[:O]
    idx5 = np.random.permutation(J)[:O]
    fk = mx_kscale(K)
    fr = mx_kscale(R)
    fl = mx_kscale(L)
    xtp = pack_weight(n((K, T)) / fk[:, None], "e4m3")
    wp = pack_weight(n((K, R)) * 1 / np.sqrt(K) * fk[:, None] * fr, "e2m1")
    wbp = pack_weight(n((R, N)) * 1 / np.sqrt(R) / fr[:, None], "e5m2")
    sxp = pack_weight(n((L, O)) / fl[:, None], "e2m1")
    wsp = pack_weight(n((L, N)) * 1 / np.sqrt(L) * fl[:, None], "e5m2")
    return {
        "xt_words": xtp[0],
        "xt_scales": xtp[1],
        "w_words": wp[0],
        "w_scales": wp[1],
        "wb_words": wbp[0],
        "wb_scales": wbp[1],
        "sx_words": sxp[0],
        "sx_scales": sxp[1],
        "ws_words": wsp[0],
        "ws_scales": wsp[1],
        "offs": striped(idx),
        "offs2": striped(idx2),
        "offs3": striped(idx3),
        "offs4": striped(idx4),
        "offs5": striped(idx5),
    }


def reference(xt_words, xt_scales, w_words, w_scales, wb_words, wb_scales, sx_words, sx_scales, ws_words, ws_scales, offs, offs2, offs3, offs4, offs5):
    idx = unstriped(offs)
    idx2 = unstriped(offs2)
    idx3 = unstriped(offs3)
    idx4 = unstriped(offs4)
    idx5 = unstriped(offs5)
    xtu = unpack_weight(xt_words, xt_scales, "e4m3")
    wu = unpack_weight(w_words, w_scales, "e2m1")
    wbu = unpack_weight(wb_words, wb_scales, "e5m2")
    sxu = unpack_weight(sx_words, sx_scales, "e2m1")
    wsu = unpack_weight(ws_words, ws_scales, "e5m2")
    xtidxg = xtu[:, idx]
    a = wu.T @ xtidxg
    xtidx2g = xtu[:, idx2]
    b = wu.T @ xtidx2g
    xtidx3g = xtu[:, idx3]
    g0 = wu.T @ xtidx3g
    c1 = np.maximum(b, g0)
    hid = np.abs(a[:, idx4] - c1[:, idx5])
    hidq = mxq(hid, 0, "e4m3")
    y = wbu.T @ hidq + wsu.T @ sxu
    return y

@@ -1,0 +1,156 @@
+from contextlib import ExitStack
+
+import concourse.mybir as mybir
+
+K, T, J, R, O, N, L = 512, 2048, 256, 512, 128, 256, 512
+FLOPS = 2 * K * R * J * 3 + 2 * R * N * O + 2 * L * N * O
+
+F32 = mybir.dt.float32
+BF16 = mybir.dt.bfloat16
+I32 = mybir.dt.int32
+U32 = mybir.dt.uint32
+U16 = mybir.dt.uint16
+U8 = mybir.dt.uint8
+E4M3 = mybir.dt.float8_e4m3fn_x4
+E5M2 = mybir.dt.float8_e5m2_x4
+E2M1 = mybir.dt.float4_e2m1fn_x4
+ALU = mybir.AluOpType
+ACT = mybir.ActivationFunctionType
+
+P = 128
+PACK = 4
+
+
+def load_scales(queues, plane, scales):
+    for r in range(4):
+        queues[r].dma_start(out=plane[r:P:32, :].bitcast(I32), in_=scales[0, r:16:4, :].bitcast(I32))
+
+
+def tile_list_triple_looked_skip_plain_kernel(
+    tc, xt_words, xt_scales, w_words, w_scales, wb_words, wb_scales, sx_words, sx_scales,
+    ws_words, ws_scales, offs, offs2, offs3, offs4, offs5, out,
+):
+    nc = tc.nc
+    with ExitStack() as ctx:
+        lists = ctx.enter_context(tc.tile_pool(name="lists", bufs=1))
+        sb = ctx.enter_context(tc.tile_pool(name="sb", bufs=1))
+        ps = ctx.enter_context(tc.psum_pool(name="ps", bufs=1))
+
+        list_a = lists.tile([P, J // 16], U16, name="list_a")
+        list_b = lists.tile([P, J // 16], U16, name="list_b")
+        list_g = lists.tile([P, J // 16], U16, name="list_g")
+        pick_a = lists.tile([P, O // 16], U16, name="pick_a")
+        pick_c = lists.tile([P, O // 16], U16, name="pick_c")
+
+        xt_w = sb.tile([P, T], I32, name="xt_w", align_bytes=64)
+        xt_s = sb.tile([P, T], U8, name="xt_s", align_bytes=64)
+        w_raw = sb.tile([P, 2 * R], U8, name="w_raw", align_bytes=64)
+        w_s_raw = sb.tile([P, R], U8, name="w_s_raw", align_bytes=64)
+        wb_w = sb.tile([P, N], I32, name="wb_w", align_bytes=64)
+        wb_s = sb.tile([P, N], U8, name="wb_s", align_bytes=64)
+        ws_w = sb.tile([P, N], I32, name="ws_w", align_bytes=64)
+        ws_s = sb.tile([P, N], U8, name="ws_s", align_bytes=64)
+        sx_w = sb.tile([P, 2 * O], U8, name="sx_w", align_bytes=64)
+        sx_s = sb.tile([P, O], U8, name="sx_s", align_bytes=64)
+
+        nc.vector.memset(xt_s[:, :1408].bitcast(I32), 0)
+        nc.gpsimd.memset(xt_s[:, 1408:].bitcast(I32), 0)
+        for plane in (w_s_raw, ws_s, sx_s, wb_s):
+            nc.gpsimd.memset(plane[:].bitcast(I32), 0)
+
+        nc.sync.dma_start(list_a[:], offs)
+        nc.sync.dma_start(list_b[:], offs2)
+        nc.sync.dma_start(list_g[:], offs3)
+        load_scales([nc.sync, nc.scalar, nc.sync, nc.scalar], xt_s, xt_scales)
+        nc.sync.dma_start(out=xt_w[:], in_=xt_words[0].rearrange("p n t -> p (n t)").bitcast(I32))
+        load_scales([nc.sync] * 4, w_s_raw, w_scales)
+        nc.sync.dma_start(out=w_raw[:].bitcast(I32), in_=w_words[0].bitcast(I32))
+        nc.sync.dma_start(pick_a[:], offs4)
+        nc.sync.dma_start(pick_c[:], offs5)
+        nc.sync.dma_start(out=ws_w[:], in_=ws_words[0].rearrange("p n t -> p (n t)").bitcast(I32))
+        nc.sync.dma_start(out=sx_w[:].bitcast(I32), in_=sx_words[0].bitcast(I32))
+        nc.sync.dma_start(out=wb_w[:], in_=wb_words[0].rearrange("p n t -> p (n t)").bitcast(I32))
+        load_scales([nc.sync] * 4, ws_s, ws_scales)
+        load_scales([nc.sync] * 4, sx_s, sx_scales)
+        load_scales([nc.sync] * 4, wb_s, wb_scales)
+
+        names = ("a", "b", "g")
+        token_lists = {"a": list_a, "b": list_b, "g": list_g}
+        x_s = {}
+        x_w = {}
+        for nm in names:
+            x_s[nm] = sb.tile([P, J], U8, name="x_s_" + nm, align_bytes=64)
+            nc.vector.tensor_copy(x_s[nm][:], xt_s[:].indirect(token_lists[nm][:]))
+
+        w_w = []
+        w_s = []
+        for t in range(PACK):
+            w_w.append(sb.tile([P, 2 * P], U8, name="w_w%d" % t, align_bytes=64))
+            w_s.append(sb.tile([P, P], U8, name="w_s%d" % t, align_bytes=64))
+            nc.scalar.copy(out=w_w[t][:].bitcast(U16), in_=w_raw[:].bitcast(U16)[:, t::PACK])
+            nc.gpsimd.tensor_copy(out=w_s[t][:], in_=w_s_raw[:, t::PACK])
+
+        for nm in names:
+            x_w[nm] = sb.tile([P, J], U32, name="x_w_" + nm, align_bytes=64)
+            nc.vector.tensor_copy(x_w[nm][:], xt_w[:].bitcast(U32).indirect(token_lists[nm][:]))
+
+        def first(nm, t, bank):
+            acc = ps.tile([P, J], F32, name="acc_%s%d" % (nm, t), tag="bank%d" % bank)
+            nc.tensor.matmul_mx(
+                out=acc[:],
+                lhsT=w_w[t][:].bitcast(E2M1),
+                lhsT_scale=w_s[t][:],
+                rhs=x_w[nm][:].bitcast(E4M3),
+                rhs_scale=x_s[nm][:],
+                start=True,
+                stop=True,
+            )
+            return acc
+
+        diff = sb.tile([P, PACK, O], F32, name="diff")
+        order = [("a", 0), ("a", 1), ("b", 0), ("b", 1), ("g", 0), ("g", 1),
+                 ("a", 2), ("b", 2), ("g", 2), ("b", 3), ("a", 3), ("g", 3)]
+        a_pick = {}
+        b_sb = {}
+        for i, (nm, t) in enumerate(order):
+            acc = first(nm, t, i % 8)
+            if nm == "a":
+                a_sb = sb.tile([P, J], F32, name="a_sb%d" % t)
+                nc.scalar.activation(out=a_sb[:], in_=acc[:], func=ACT.Copy)
+                a_pick[t] = sb.tile([P, O], F32, name="a_pick%d" % t)
+                nc.scalar.activation(out=a_pick[t][:], in_=a_sb[:].indirect(pick_a[:]), func=ACT.Copy)
+            elif nm == "b":
+                b_sb[t] = sb.tile([P, J], F32, name="b_sb%d" % t)
+                if t == 0:
+                    nc.vector.tensor_copy(b_sb[t][:], acc[:])
+                else:
+                    nc.scalar.activation(out=b_sb[t][:], in_=acc[:], func=ACT.Copy)
+            else:
+                c1 = sb.tile([P, J], F32, name="c1_%d" % t)
+                nc.vector.tensor_tensor(c1[:], acc[:], b_sb[t][:], ALU.max)
+                nc.vector.tensor_tensor(diff[:, t, :], c1[:].indirect(pick_c[:]), a_pick[t][:], ALU.subtract)
+
+        hid = sb.tile([P, O, PACK], BF16, name="hid", align_bytes=64)
+        half = O // 2
+        nc.scalar.activation(out=hid[:, :half, :], in_=diff[:, :, :half].rearrange("p t o -> p o t"), func=ACT.Abs)
+        rest = diff[:, :, half:].rearrange("p t o -> p o t")
+        nc.vector.scalar_tensor_tensor(hid[:, half:, :], rest, -1.0, rest, ALU.mult, ALU.max)
+
+        hid_w = sb.tile([P, O], U32, name="hid_w", align_bytes=64)
+        hid_s = sb.tile([P, O], U8, name="hid_s", align_bytes=64)
+        nc.vector.quantize_mx(out=hid_w[:].bitcast(E4M3), scales=hid_s[:], in_=hid[:].rearrange("p o t -> p (o t)"))
+
+        for h in range(2):
+            cols = slice(P * h, P * (h + 1))
+            y = ps.tile([P, O], F32, name="y%d" % h, tag="bank%d" % (4 + h))
+            nc.tensor.matmul_mx(out=y[:], lhsT=ws_w[:, cols].bitcast(E5M2), lhsT_scale=ws_s[:, cols],
+                                rhs=sx_w[:].bitcast(E2M1), rhs_scale=sx_s[:], start=True, stop=False)
+            nc.tensor.matmul_mx(out=y[:], lhsT=wb_w[:, cols].bitcast(E5M2), lhsT_scale=wb_s[:, cols],
+                                rhs=hid_w[:].bitcast(E4M3), rhs_scale=hid_s[:], start=False, stop=True)
+            y_sb = sb.tile([P, O], F32, name="y_sb%d" % h)
+            if h == 0:
+                nc.vector.tensor_copy(y_sb[:], y[:])
+                nc.sync.dma_start(out=out[cols, :], in_=y_sb[:])
+            else:
+                nc.scalar.activation(out=y_sb[:], in_=y[:], func=ACT.Copy)
+                nc.scalar.dma_start(out=out[cols, :], in_=y_sb[:])

@@ -45,7 +45,7 @@ def tile_list_triple_looked_skip_plain_kernel(
         xt_w = sb.tile([P, T], I32, name="xt_w", align_bytes=64)
         xt_s = sb.tile([P, T], U8, name="xt_s", align_bytes=64)
         w_raw = sb.tile([P, 2 * R], U8, name="w_raw", align_bytes=64)
-        w_s_raw = sb.tile([P, R], U8, name="w_s_raw", align_bytes=64)
+        w_s_raw = sb.tile([P, R], U8, name="w_s_raw", tag="shared", align_bytes=64)
         wb_w = sb.tile([P, N], I32, name="wb_w", align_bytes=64)
         wb_s = sb.tile([P, N], U8, name="wb_s", align_bytes=64)
         ws_w = sb.tile([P, N], I32, name="ws_w", align_bytes=64)
@@ -82,25 +82,33 @@ def tile_list_triple_looked_skip_plain_kernel(
             x_s[nm] = sb.tile([P, J], U8, name="x_s_" + nm, align_bytes=64)
             nc.vector.tensor_copy(x_s[nm][:], xt_s[:].indirect(token_lists[nm][:]))
 
+        def gather_words(nm, dst):
+            x_w[nm] = dst
+            nc.vector.tensor_copy(dst, xt_w[:].bitcast(U32).indirect(token_lists[nm][:]))
+
         w_w = []
-        w_s = []
         for t in range(PACK):
             w_w.append(sb.tile([P, 2 * P], U8, name="w_w%d" % t, align_bytes=64))
-            w_s.append(sb.tile([P, P], U8, name="w_s%d" % t, align_bytes=64))
             nc.scalar.copy(out=w_w[t][:].bitcast(U16), in_=w_raw[:].bitcast(U16)[:, t::PACK])
-            nc.gpsimd.tensor_copy(out=w_s[t][:], in_=w_s_raw[:, t::PACK])
 
-        for nm in names:
-            x_w[nm] = sb.tile([P, J], U32, name="x_w_" + nm, align_bytes=64)
-            nc.vector.tensor_copy(x_w[nm][:], xt_w[:].bitcast(U32).indirect(token_lists[nm][:]))
+        x_w_a = sb.tile([P, J], U32, name="x_w_a", align_bytes=64)
+        gather_words("a", x_w_a[:])
+        w_s = sb.tile([P, R], U8, name="w_s", align_bytes=64)
+        nc.vector.tensor_copy(
+            out=w_s[:].rearrange("p (t m) -> p t m", t=PACK),
+            in_=w_s_raw[:].rearrange("p (m t) -> p t m", t=PACK),
+        )
+        x_w_bg = sb.tile([P, 2 * J], U32, name="x_w_bg", tag="shared", align_bytes=64)
+        gather_words("b", x_w_bg[:, :J])
+        gather_words("g", x_w_bg[:, J:])
 
         def first(nm, t, bank):
             acc = ps.tile([P, J], F32, name="acc_%s%d" % (nm, t), tag="bank%d" % bank)
             nc.tensor.matmul_mx(
                 out=acc[:],
                 lhsT=w_w[t][:].bitcast(E2M1),
-                lhsT_scale=w_s[t][:],
-                rhs=x_w[nm][:].bitcast(E4M3),
+                lhsT_scale=w_s[:, P * t : P * (t + 1)],
+                rhs=x_w[nm].bitcast(E4M3),
                 rhs_scale=x_s[nm][:],
                 start=True,
                 stop=True,
@@ -108,31 +116,66 @@ def tile_list_triple_looked_skip_plain_kernel(
             return acc
 
         diff = sb.tile([P, PACK, O], F32, name="diff")
-        order = [("a", 0), ("a", 1), ("b", 0), ("b", 1), ("g", 0), ("g", 1),
-                 ("a", 2), ("b", 2), ("g", 2), ("b", 3), ("a", 3), ("g", 3)]
+        acc = {}
+        a_sb = {}
         a_pick = {}
         b_sb = {}
-        for i, (nm, t) in enumerate(order):
-            acc = first(nm, t, i % 8)
-            if nm == "a":
-                a_sb = sb.tile([P, J], F32, name="a_sb%d" % t)
-                nc.scalar.activation(out=a_sb[:], in_=acc[:], func=ACT.Copy)
-                a_pick[t] = sb.tile([P, O], F32, name="a_pick%d" % t)
-                nc.scalar.activation(out=a_pick[t][:], in_=a_sb[:].indirect(pick_a[:]), func=ACT.Copy)
-            elif nm == "b":
-                b_sb[t] = sb.tile([P, J], F32, name="b_sb%d" % t)
-                if t == 0:
-                    nc.vector.tensor_copy(b_sb[t][:], acc[:])
-                else:
-                    nc.scalar.activation(out=b_sb[t][:], in_=acc[:], func=ACT.Copy)
+        c1 = {}
+
+        def product(nm, t):
+            acc[nm, t] = first(nm, t, len(acc) % 8)
+
+        def take_a(t):
+            a_sb[t] = sb.tile([P, J], F32, name="a_sb%d" % t)
+            nc.scalar.activation(out=a_sb[t][:], in_=acc["a", t][:], func=ACT.Copy)
+
+        def take_b(t):
+            b_sb[t] = sb.tile([P, J], F32, name="b_sb%d" % t)
+            if t == 0:
+                nc.vector.tensor_copy(b_sb[t][:], acc["b", t][:])
             else:
-                c1 = sb.tile([P, J], F32, name="c1_%d" % t)
-                nc.vector.tensor_tensor(c1[:], acc[:], b_sb[t][:], ALU.max)
-                nc.vector.tensor_tensor(diff[:, t, :], c1[:].indirect(pick_c[:]), a_pick[t][:], ALU.subtract)
+                nc.scalar.activation(out=b_sb[t][:], in_=acc["b", t][:], func=ACT.Copy)
+
+        def look_a(t):
+            a_pick[t] = sb.tile([P, O], F32, name="a_pick%d" % t)
+            nc.scalar.activation(out=a_pick[t][:], in_=a_sb[t][:].indirect(pick_a[:]), func=ACT.Copy)
+
+        def larger(t):
+            c1[t] = sb.tile([P, J], F32, name="c1_%d" % t)
+            nc.vector.tensor_tensor(c1[t][:], acc["g", t][:], b_sb[t][:], ALU.max)
+
+        def look_c(t):
+            nc.vector.tensor_tensor(diff[:, t, :], c1[t][:].indirect(pick_c[:]), a_pick[t][:], ALU.subtract)
+
+        for nm in names:
+            product(nm, 0)
+            product(nm, 1)
+        take_a(0)
+        take_a(1)
+        take_b(0)
+        look_a(0)
+        take_b(1)
+        look_a(1)
+        larger(0)
+        larger(1)
+        look_c(0)
+        look_c(1)
+        for t in (2, 3):
+            for nm in names:
+                product(nm, t)
+            take_a(t)
+            take_b(t)
+            look_a(t)
+            larger(t)
+            look_c(t)
 
         hid = sb.tile([P, O, PACK], BF16, name="hid", align_bytes=64)
         half = O // 2
-        nc.scalar.activation(out=hid[:, :half, :], in_=diff[:, :, :half].rearrange("p t o -> p o t"), func=ACT.Abs)
+        nc.scalar.activation(
+            out=hid[:, :half, :].rearrange("p (c i) t -> p c t i", i=4),
+            in_=diff[:, :, :half].rearrange("p t (c i) -> p c t i", i=4),
+            func=ACT.Abs,
+        )
         rest = diff[:, :, half:].rearrange("p t o -> p o t")
         nc.vector.scalar_tensor_tensor(hid[:, half:, :], rest, -1.0, rest, ALU.mult, ALU.max)
 

@@ -45,7 +45,7 @@ def tile_list_triple_looked_skip_plain_kernel(
         xt_w = sb.tile([P, T], I32, name="xt_w", align_bytes=64)
         xt_s = sb.tile([P, T], U8, name="xt_s", align_bytes=64)
         w_raw = sb.tile([P, 2 * R], U8, name="w_raw", align_bytes=64)
-        w_s_raw = sb.tile([P, R], U8, name="w_s_raw", tag="shared", align_bytes=64)
+        w_s_raw = sb.tile([P, R], U8, name="w_s_raw", align_bytes=64)
         wb_w = sb.tile([P, N], I32, name="wb_w", align_bytes=64)
         wb_s = sb.tile([P, N], U8, name="wb_s", align_bytes=64)
         ws_w = sb.tile([P, N], I32, name="ws_w", align_bytes=64)
@@ -82,33 +82,35 @@ def tile_list_triple_looked_skip_plain_kernel(
             x_s[nm] = sb.tile([P, J], U8, name="x_s_" + nm, align_bytes=64)
             nc.vector.tensor_copy(x_s[nm][:], xt_s[:].indirect(token_lists[nm][:]))
 
-        def gather_words(nm, dst):
-            x_w[nm] = dst
-            nc.vector.tensor_copy(dst, xt_w[:].bitcast(U32).indirect(token_lists[nm][:]))
-
         w_w = []
-        for t in range(PACK):
-            w_w.append(sb.tile([P, 2 * P], U8, name="w_w%d" % t, align_bytes=64))
-            nc.scalar.copy(out=w_w[t][:].bitcast(U16), in_=w_raw[:].bitcast(U16)[:, t::PACK])
+        w_s = []
+        for u in range(2):
+            pair = slice(2 * u, 2 * u + 2)
+            words = sb.tile([P, 4 * P], U8, name="w_w%d" % u, align_bytes=64)
+            plane = sb.tile([P, 2 * P], U8, name="w_s%d" % u, align_bytes=64)
+            nc.scalar.copy(
+                out=words[:].bitcast(U16).rearrange("p (t m) -> p t m", t=2),
+                in_=w_raw[:].bitcast(U16).rearrange("p (m t) -> p t m", t=PACK)[:, pair, :],
+            )
+            nc.gpsimd.tensor_copy(
+                out=plane[:].rearrange("p (t m) -> p t m", t=2),
+                in_=w_s_raw[:].rearrange("p (m t) -> p t m", t=PACK)[:, pair, :],
+            )
+            for e in range(2):
+                w_w.append(words[:, 2 * P * e : 2 * P * (e + 1)])
+                w_s.append(plane[:, P * e : P * (e + 1)])
 
-        x_w_a = sb.tile([P, J], U32, name="x_w_a", align_bytes=64)
-        gather_words("a", x_w_a[:])
-        w_s = sb.tile([P, R], U8, name="w_s", align_bytes=64)
-        nc.vector.tensor_copy(
-            out=w_s[:].rearrange("p (t m) -> p t m", t=PACK),
-            in_=w_s_raw[:].rearrange("p (m t) -> p t m", t=PACK),
-        )
-        x_w_bg = sb.tile([P, 2 * J], U32, name="x_w_bg", tag="shared", align_bytes=64)
-        gather_words("b", x_w_bg[:, :J])
-        gather_words("g", x_w_bg[:, J:])
+        for nm in names:
+            x_w[nm] = sb.tile([P, J], U32, name="x_w_" + nm, align_bytes=64)
+            nc.vector.tensor_copy(x_w[nm][:], xt_w[:].bitcast(U32).indirect(token_lists[nm][:]))
 
         def first(nm, t, bank):
             acc = ps.tile([P, J], F32, name="acc_%s%d" % (nm, t), tag="bank%d" % bank)
             nc.tensor.matmul_mx(
                 out=acc[:],
-                lhsT=w_w[t][:].bitcast(E2M1),
-                lhsT_scale=w_s[:, P * t : P * (t + 1)],
-                rhs=x_w[nm].bitcast(E4M3),
+                lhsT=w_w[t].bitcast(E2M1),
+                lhsT_scale=w_s[t],
+                rhs=x_w[nm][:].bitcast(E4M3),
                 rhs_scale=x_s[nm][:],
                 start=True,
                 stop=True,
@@ -131,7 +133,7 @@ def tile_list_triple_looked_skip_plain_kernel(
 
         def take_b(t):
             b_sb[t] = sb.tile([P, J], F32, name="b_sb%d" % t)
-            if t == 0:
+            if t < 2:
                 nc.vector.tensor_copy(b_sb[t][:], acc["b", t][:])
             else:
                 nc.scalar.activation(out=b_sb[t][:], in_=acc["b", t][:], func=ACT.Copy)
@@ -148,25 +150,21 @@ def tile_list_triple_looked_skip_plain_kernel(
             nc.vector.tensor_tensor(diff[:, t, :], c1[t][:].indirect(pick_c[:]), a_pick[t][:], ALU.subtract)
 
         for nm in names:
-            product(nm, 0)
-            product(nm, 1)
-        take_a(0)
-        take_a(1)
-        take_b(0)
-        look_a(0)
-        take_b(1)
-        look_a(1)
-        larger(0)
-        larger(1)
-        look_c(0)
-        look_c(1)
-        for t in (2, 3):
-            for nm in names:
+            for t in (0, 1):
                 product(nm, t)
-            take_a(t)
+        for step in (take_a, look_a, take_b, larger):
+            for t in (0, 1):
+                step(t)
+        for t in (2, 3):
+            for nm in ("b", "a", "g"):
+                product(nm, t)
             take_b(t)
+            take_a(t)
+        for t in (2, 3):
             look_a(t)
+            look_c(t - 2)
             larger(t)
+        for t in (2, 3):
             look_c(t)
 
         hid = sb.tile([P, O, PACK], BF16, name="hid", align_bytes=64)

@@ -53,8 +53,7 @@ def tile_list_triple_looked_skip_plain_kernel(
         sx_w = sb.tile([P, 2 * O], U8, name="sx_w", align_bytes=64)
         sx_s = sb.tile([P, O], U8, name="sx_s", align_bytes=64)
 
-        nc.vector.memset(xt_s[:, :1408].bitcast(I32), 0)
-        nc.gpsimd.memset(xt_s[:, 1408:].bitcast(I32), 0)
+        nc.vector.memset(xt_s[:].bitcast(I32), 0)
         for plane in (w_s_raw, ws_s, sx_s, wb_s):
             nc.gpsimd.memset(plane[:].bitcast(I32), 0)
 
@@ -168,7 +167,7 @@ def tile_list_triple_looked_skip_plain_kernel(
             look_c(t)
 
         hid = sb.tile([P, O, PACK], BF16, name="hid", align_bytes=64)
-        half = O // 2
+        half = 88
         nc.scalar.activation(
             out=hid[:, :half, :].rearrange("p (c i) t -> p c t i", i=4),
             in_=diff[:, :, :half].rearrange("p t (c i) -> p c t i", i=4),

from contextlib import ExitStack

import concourse.mybir as mybir

K, T, J, R, O, N, L = 512, 2048, 256, 512, 128, 256, 512
FLOPS = 2 * K * R * J * 3 + 2 * R * N * O + 2 * L * N * O

F32 = mybir.dt.float32
BF16 = mybir.dt.bfloat16
I32 = mybir.dt.int32
U32 = mybir.dt.uint32
U16 = mybir.dt.uint16
U8 = mybir.dt.uint8
E4M3 = mybir.dt.float8_e4m3fn_x4
E5M2 = mybir.dt.float8_e5m2_x4
E2M1 = mybir.dt.float4_e2m1fn_x4
ALU = mybir.AluOpType
ACT = mybir.ActivationFunctionType

P = 128
PACK = 4


def load_scales(queues, plane, scales):
    for r in range(4):
        queues[r].dma_start(out=plane[r:P:32, :].bitcast(I32), in_=scales[0, r:16:4, :].bitcast(I32))


def tile_list_triple_looked_skip_plain_kernel(
    tc, xt_words, xt_scales, w_words, w_scales, wb_words, wb_scales, sx_words, sx_scales,
    ws_words, ws_scales, offs, offs2, offs3, offs4, offs5, out,
):
    nc = tc.nc
    with ExitStack() as ctx:
        lists = ctx.enter_context(tc.tile_pool(name="lists", bufs=1))
        sb = ctx.enter_context(tc.tile_pool(name="sb", bufs=1))
        ps = ctx.enter_context(tc.psum_pool(name="ps", bufs=1))

        list_a = lists.tile([P, J // 16], U16, name="list_a")
        list_b = lists.tile([P, J // 16], U16, name="list_b")
        list_g = lists.tile([P, J // 16], U16, name="list_g")
        pick_a = lists.tile([P, O // 16], U16, name="pick_a")
        pick_c = lists.tile([P, O // 16], U16, name="pick_c")

        xt_w = sb.tile([P, T], I32, name="xt_w", align_bytes=64)
        xt_s = sb.tile([P, T], U8, name="xt_s", align_bytes=64)
        w_raw = sb.tile([P, 2 * R], U8, name="w_raw", align_bytes=64)
        w_s_raw = sb.tile([P, R], U8, name="w_s_raw", align_bytes=64)
        wb_w = sb.tile([P, N], I32, name="wb_w", align_bytes=64)
        wb_s = sb.tile([P, N], U8, name="wb_s", align_bytes=64)
        ws_w = sb.tile([P, N], I32, name="ws_w", align_bytes=64)
        ws_s = sb.tile([P, N], U8, name="ws_s", align_bytes=64)
        sx_w = sb.tile([P, 2 * O], U8, name="sx_w", align_bytes=64)
        sx_s = sb.tile([P, O], U8, name="sx_s", align_bytes=64)

        nc.vector.memset(xt_s[:].bitcast(I32), 0)
        for plane in (w_s_raw, ws_s, sx_s, wb_s):
            nc.gpsimd.memset(plane[:].bitcast(I32), 0)

        nc.sync.dma_start(list_a[:], offs)
        nc.sync.dma_start(list_b[:], offs2)
        nc.sync.dma_start(list_g[:], offs3)
        load_scales([nc.sync, nc.scalar, nc.sync, nc.scalar], xt_s, xt_scales)
        nc.sync.dma_start(out=xt_w[:], in_=xt_words[0].rearrange("p n t -> p (n t)").bitcast(I32))
        load_scales([nc.sync] * 4, w_s_raw, w_scales)
        nc.sync.dma_start(out=w_raw[:].bitcast(I32), in_=w_words[0].bitcast(I32))
        nc.sync.dma_start(pick_a[:], offs4)
        nc.sync.dma_start(pick_c[:], offs5)
        nc.sync.dma_start(out=ws_w[:], in_=ws_words[0].rearrange("p n t -> p (n t)").bitcast(I32))
        nc.sync.dma_start(out=sx_w[:].bitcast(I32), in_=sx_words[0].bitcast(I32))
        nc.sync.dma_start(out=wb_w[:], in_=wb_words[0].rearrange("p n t -> p (n t)").bitcast(I32))
        load_scales([nc.sync] * 4, ws_s, ws_scales)
        load_scales([nc.sync] * 4, sx_s, sx_scales)
        load_scales([nc.sync] * 4, wb_s, wb_scales)

        names = ("a", "b", "g")
        token_lists = {"a": list_a, "b": list_b, "g": list_g}
        x_s = {}
        x_w = {}
        for nm in names:
            x_s[nm] = sb.tile([P, J], U8, name="x_s_" + nm, align_bytes=64)
            nc.vector.tensor_copy(x_s[nm][:], xt_s[:].indirect(token_lists[nm][:]))

        w_w = []
        w_s = []
        for u in range(2):
            pair = slice(2 * u, 2 * u + 2)
            words = sb.tile([P, 4 * P], U8, name="w_w%d" % u, align_bytes=64)
            plane = sb.tile([P, 2 * P], U8, name="w_s%d" % u, align_bytes=64)
            nc.scalar.copy(
                out=words[:].bitcast(U16).rearrange("p (t m) -> p t m", t=2),
                in_=w_raw[:].bitcast(U16).rearrange("p (m t) -> p t m", t=PACK)[:, pair, :],
            )
            nc.gpsimd.tensor_copy(
                out=plane[:].rearrange("p (t m) -> p t m", t=2),
                in_=w_s_raw[:].rearrange("p (m t) -> p t m", t=PACK)[:, pair, :],
            )
            for e in range(2):
                w_w.append(words[:, 2 * P * e : 2 * P * (e + 1)])
                w_s.append(plane[:, P * e : P * (e + 1)])

        for nm in names:
            x_w[nm] = sb.tile([P, J], U32, name="x_w_" + nm, align_bytes=64)
            nc.vector.tensor_copy(x_w[nm][:], xt_w[:].bitcast(U32).indirect(token_lists[nm][:]))

        def first(nm, t, bank):
            acc = ps.tile([P, J], F32, name="acc_%s%d" % (nm, t), tag="bank%d" % bank)
            nc.tensor.matmul_mx(
                out=acc[:],
                lhsT=w_w[t].bitcast(E2M1),
                lhsT_scale=w_s[t],
                rhs=x_w[nm][:].bitcast(E4M3),
                rhs_scale=x_s[nm][:],
                start=True,
                stop=True,
            )
            return acc

        diff = sb.tile([P, PACK, O], F32, name="diff")
        acc = {}
        a_sb = {}
        a_pick = {}
        b_sb = {}
        c1 = {}

        def product(nm, t):
            acc[nm, t] = first(nm, t, len(acc) % 8)

        def take_a(t):
            a_sb[t] = sb.tile([P, J], F32, name="a_sb%d" % t)
            nc.scalar.activation(out=a_sb[t][:], in_=acc["a", t][:], func=ACT.Copy)

        def take_b(t):
            b_sb[t] = sb.tile([P, J], F32, name="b_sb%d" % t)
            if t < 2:
                nc.vector.tensor_copy(b_sb[t][:], acc["b", t][:])
            else:
                nc.scalar.activation(out=b_sb[t][:], in_=acc["b", t][:], func=ACT.Copy)

        def look_a(t):
            a_pick[t] = sb.tile([P, O], F32, name="a_pick%d" % t)
            nc.scalar.activation(out=a_pick[t][:], in_=a_sb[t][:].indirect(pick_a[:]), func=ACT.Copy)

        def larger(t):
            c1[t] = sb.tile([P, J], F32, name="c1_%d" % t)
            nc.vector.tensor_tensor(c1[t][:], acc["g", t][:], b_sb[t][:], ALU.max)

        def look_c(t):
            nc.vector.tensor_tensor(diff[:, t, :], c1[t][:].indirect(pick_c[:]), a_pick[t][:], ALU.subtract)

        for nm in names:
            for t in (0, 1):
                product(nm, t)
        for step in (take_a, look_a, take_b, larger):
            for t in (0, 1):
                step(t)
        for t in (2, 3):
            for nm in ("b", "a", "g"):
                product(nm, t)
            take_b(t)
            take_a(t)
        for t in (2, 3):
            look_a(t)
            look_c(t - 2)
            larger(t)
        for t in (2, 3):
            look_c(t)

        hid = sb.tile([P, O, PACK], BF16, name="hid", align_bytes=64)
        half = 88
        nc.scalar.activation(
            out=hid[:, :half, :].rearrange("p (c i) t -> p c t i", i=4),
            in_=diff[:, :, :half].rearrange("p t (c i) -> p c t i", i=4),
            func=ACT.Abs,
        )
        rest = diff[:, :, half:].rearrange("p t o -> p o t")
        nc.vector.scalar_tensor_tensor(hid[:, half:, :], rest, -1.0, rest, ALU.mult, ALU.max)

        hid_w = sb.tile([P, O], U32, name="hid_w", align_bytes=64)
        hid_s = sb.tile([P, O], U8, name="hid_s", align_bytes=64)
        nc.vector.quantize_mx(out=hid_w[:].bitcast(E4M3), scales=hid_s[:], in_=hid[:].rearrange("p o t -> p (o t)"))

        for h in range(2):
            cols = slice(P * h, P * (h + 1))
            y = ps.tile([P, O], F32, name="y%d" % h, tag="bank%d" % (4 + h))
            nc.tensor.matmul_mx(out=y[:], lhsT=ws_w[:, cols].bitcast(E5M2), lhsT_scale=ws_s[:, cols],
                                rhs=sx_w[:].bitcast(E2M1), rhs_scale=sx_s[:], start=True, stop=False)
            nc.tensor.matmul_mx(out=y[:], lhsT=wb_w[:, cols].bitcast(E5M2), lhsT_scale=wb_s[:, cols],
                                rhs=hid_w[:].bitcast(E4M3), rhs_scale=hid_s[:], start=False, stop=True)
            y_sb = sb.tile([P, O], F32, name="y_sb%d" % h)
            if h == 0:
                nc.vector.tensor_copy(y_sb[:], y[:])
                nc.sync.dma_start(out=out[cols, :], in_=y_sb[:])
            else:
                nc.scalar.activation(out=y_sb[:], in_=y[:], func=ACT.Copy)
                nc.scalar.dma_start(out=out[cols, :], in_=y_sb[:])
